import numpy as np
import ml_dtypes

BF16 = ml_dtypes.bfloat16


def bf(x):
    return np.asarray(x, np.float32).astype(BF16)


def f32(x):
    return np.asarray(x, np.float32)


def f64(x):
    return np.asarray(x).astype(np.float64)


def striped(idx):
    return np.tile(idx.reshape(-1, 16).T, (8, 1))


S, K, M, N, D, V = 1024, 256, 256, 192, 8, 24


def setup_inputs():
    return {"table": bf(np.random.standard_normal((K, S))), "w": bf(np.random.standard_normal((K, M)) / np.sqrt(K)), "b": f32(0.5 * np.random.standard_normal((M, 1))), "offs": striped(np.random.permutation(np.tile(np.arange(S), 2))[:N])}


def reference(table, w, b, offs):
    idx = offs[:16].T.reshape(-1)
    x = f64(table)[:, idx]
    y = f64(w).T @ x
    z = np.tanh(y + f64(b))
    return z.reshape(M, V, D).mean(axis=2)

@@ -1,0 +1,63 @@
+import concourse.mybir as mybir
+
+BF16 = mybir.dt.bfloat16
+F32 = mybir.dt.float32
+U16 = mybir.dt.uint16
+
+P = 128
+S = 1024
+K = 256
+M = 256
+N = 192
+D = 8
+V = N // D
+K_BLOCKS = K // P
+M_BLOCKS = M // P
+
+FLOPS = 2 * K * M * N
+
+
+def tile_gather_matmul_kernel(tc, table, w, b, offs, out):
+    nc = tc.nc
+    with (
+        tc.tile_pool(name="held", bufs=1) as held,
+        tc.psum_pool(name="banks", bufs=1) as banks,
+    ):
+        offsets = held.tile([P, N // 16], U16, name="offsets")
+        nc.sync.dma_start(offsets[:], offs)
+
+        table_blocks = [held.tile([P, S], BF16, name=f"table{k}") for k in range(K_BLOCKS)]
+        for k in range(K_BLOCKS):
+            nc.sync.dma_start(table_blocks[k][:], table[k * P : (k + 1) * P, :])
+
+        weights = held.tile([P, K_BLOCKS, M], BF16, name="weights")
+        nc.scalar.dma_start(weights[:], w.rearrange("(k p) m -> p k m", p=P))
+
+        bias = held.tile([P, M_BLOCKS], F32, name="bias")
+        with nc.allow_non_contiguous_dma(reason="one float32 to a partition for each block of b"):
+            nc.scalar.dma_start(bias[:], b.rearrange("(a p) o -> p (a o)", p=P))
+
+        pooled = held.tile([P, M_BLOCKS, V], F32, name="pooled")
+        for a in range(M_BLOCKS):
+            bank = banks.tile([P, N], F32, name=f"bank{a}")
+            for k in range(K_BLOCKS):
+                nc.tensor.matmul(
+                    bank[:],
+                    weights[:, k, a * P : (a + 1) * P],
+                    table_blocks[k][:].indirect(offsets[:]),
+                    start=(k == 0),
+                    stop=(k == K_BLOCKS - 1),
+                )
+            z = held.tile([P, N], F32, name=f"z{a}")
+            nc.scalar.activation(
+                z[:], bank[:], mybir.ActivationFunctionType.Tanh, bias=bias[:, a : a + 1]
+            )
+            nc.vector.tensor_reduce(
+                pooled[:, a, :],
+                z[:].rearrange("p (v t) -> p v t", t=D),
+                axis=mybir.AxisListType.X,
+                op=mybir.AluOpType.add,
+            )
+
+        nc.vector.tensor_scalar_mul(pooled[:], pooled[:], 1.0 / D)
+        nc.sync.dma_start(out.rearrange("(a p) v -> p a v", p=P), pooled[:])

@@ -19,6 +19,7 @@ FLOPS = 2 * K * M * N
 
 def tile_gather_matmul_kernel(tc, table, w, b, offs, out):
     nc = tc.nc
+    tanh = mybir.ActivationFunctionType.Tanh
     with (
         tc.tile_pool(name="held", bufs=1) as held,
         tc.psum_pool(name="banks", bufs=1) as banks,
@@ -27,31 +28,35 @@ def tile_gather_matmul_kernel(tc, table, w, b, offs, out):
         nc.sync.dma_start(offsets[:], offs)
 
         table_blocks = [held.tile([P, S], BF16, name=f"table{k}") for k in range(K_BLOCKS)]
-        for k in range(K_BLOCKS):
-            nc.sync.dma_start(table_blocks[k][:], table[k * P : (k + 1) * P, :])
-
-        weights = held.tile([P, K_BLOCKS, M], BF16, name="weights")
-        nc.scalar.dma_start(weights[:], w.rearrange("(k p) m -> p k m", p=P))
+        weight_blocks = [held.tile([P, M], BF16, name=f"weights{k}") for k in range(K_BLOCKS)]
+        nc.scalar.dma_start(weight_blocks[0][:], w[0:P, :])
+        nc.sync.dma_start(table_blocks[0][:], table[0:P, :])
+        nc.sync.dma_start(weight_blocks[1][:], w[P : 2 * P, :])
+        nc.sync.dma_start(table_blocks[1][:], table[P : 2 * P, :])
 
         bias = held.tile([P, M_BLOCKS], F32, name="bias")
         with nc.allow_non_contiguous_dma(reason="one float32 to a partition for each block of b"):
             nc.scalar.dma_start(bias[:], b.rearrange("(a p) o -> p (a o)", p=P))
 
-        pooled = held.tile([P, M_BLOCKS, V], F32, name="pooled")
-        for a in range(M_BLOCKS):
-            bank = banks.tile([P, N], F32, name=f"bank{a}")
-            for k in range(K_BLOCKS):
+        scratch = held.tile([P, 1], F32, name="scratch")
+        nc.vector.memset(scratch[:], 0.0)
+        nc.scalar.activation(scratch[:], scratch[:], tanh)
+
+        bank_tiles = [banks.tile([P, N], F32, name=f"bank{a}") for a in range(M_BLOCKS)]
+        for k in range(K_BLOCKS):
+            for a in range(M_BLOCKS):
                 nc.tensor.matmul(
-                    bank[:],
-                    weights[:, k, a * P : (a + 1) * P],
+                    bank_tiles[a][:],
+                    weight_blocks[k][:, a * P : (a + 1) * P],
                     table_blocks[k][:].indirect(offsets[:]),
                     start=(k == 0),
                     stop=(k == K_BLOCKS - 1),
                 )
+
+        pooled = held.tile([P, M_BLOCKS, V], F32, name="pooled")
+        for a in range(M_BLOCKS):
             z = held.tile([P, N], F32, name=f"z{a}")
-            nc.scalar.activation(
-                z[:], bank[:], mybir.ActivationFunctionType.Tanh, bias=bias[:, a : a + 1]
-            )
+            nc.scalar.activation(z[:], bank_tiles[a][:], tanh, bias=bias[:, a : a + 1])
             nc.vector.tensor_reduce(
                 pooled[:, a, :],
                 z[:].rearrange("p (v t) -> p v t", t=D),

@@ -16,6 +16,9 @@ M_BLOCKS = M // P
 
 FLOPS = 2 * K * M * N
 
+WARM_COLUMNS = 256
+WARM_MATMULS = 8
+
 
 def tile_gather_matmul_kernel(tc, table, w, b, offs, out):
     nc = tc.nc
@@ -38,9 +41,13 @@ def tile_gather_matmul_kernel(tc, table, w, b, offs, out):
         with nc.allow_non_contiguous_dma(reason="one float32 to a partition for each block of b"):
             nc.scalar.dma_start(bias[:], b.rearrange("(a p) o -> p (a o)", p=P))
 
+        zeros = held.tile([P, WARM_COLUMNS], BF16, name="zeros")
+        nc.vector.memset(zeros[:], 0.0)
         scratch = held.tile([P, 1], F32, name="scratch")
-        nc.vector.memset(scratch[:], 0.0)
-        nc.scalar.activation(scratch[:], scratch[:], tanh)
+        nc.scalar.activation(scratch[:], zeros[:, 0:1], tanh)
+        warm_bank = banks.tile([P, WARM_COLUMNS], F32, name="warm_bank")
+        for i in range(WARM_MATMULS):
+            nc.tensor.matmul(warm_bank[:], zeros[:, 0:P], zeros[:], start=True, stop=True)
 
         bank_tiles = [banks.tile([P, N], F32, name=f"bank{a}") for a in range(M_BLOCKS)]
         for k in range(K_BLOCKS):

@@ -16,9 +16,6 @@ M_BLOCKS = M // P
 
 FLOPS = 2 * K * M * N
 
-WARM_COLUMNS = 256
-WARM_MATMULS = 8
-
 
 def tile_gather_matmul_kernel(tc, table, w, b, offs, out):
     nc = tc.nc
@@ -30,6 +27,10 @@ def tile_gather_matmul_kernel(tc, table, w, b, offs, out):
         offsets = held.tile([P, N // 16], U16, name="offsets")
         nc.sync.dma_start(offsets[:], offs)
 
+        bias = held.tile([P, M_BLOCKS], F32, name="bias")
+        with nc.allow_non_contiguous_dma(reason="one float32 to a partition for each block of b"):
+            nc.scalar.dma_start(bias[:], b.rearrange("(a p) o -> p (a o)", p=P))
+
         table_blocks = [held.tile([P, S], BF16, name=f"table{k}") for k in range(K_BLOCKS)]
         weight_blocks = [held.tile([P, M], BF16, name=f"weights{k}") for k in range(K_BLOCKS)]
         nc.scalar.dma_start(weight_blocks[0][:], w[0:P, :])
@@ -37,17 +38,9 @@ def tile_gather_matmul_kernel(tc, table, w, b, offs, out):
         nc.sync.dma_start(weight_blocks[1][:], w[P : 2 * P, :])
         nc.sync.dma_start(table_blocks[1][:], table[P : 2 * P, :])
 
-        bias = held.tile([P, M_BLOCKS], F32, name="bias")
-        with nc.allow_non_contiguous_dma(reason="one float32 to a partition for each block of b"):
-            nc.scalar.dma_start(bias[:], b.rearrange("(a p) o -> p (a o)", p=P))
-
-        zeros = held.tile([P, WARM_COLUMNS], BF16, name="zeros")
-        nc.vector.memset(zeros[:], 0.0)
         scratch = held.tile([P, 1], F32, name="scratch")
-        nc.scalar.activation(scratch[:], zeros[:, 0:1], tanh)
-        warm_bank = banks.tile([P, WARM_COLUMNS], F32, name="warm_bank")
-        for i in range(WARM_MATMULS):
-            nc.tensor.matmul(warm_bank[:], zeros[:, 0:P], zeros[:], start=True, stop=True)
+        nc.vector.memset(scratch[:], 0.0)
+        nc.scalar.activation(scratch[:], scratch[:], tanh)
 
         bank_tiles = [banks.tile([P, N], F32, name=f"bank{a}") for a in range(M_BLOCKS)]
         for k in range(K_BLOCKS):
@@ -60,16 +53,15 @@ def tile_gather_matmul_kernel(tc, table, w, b, offs, out):
                     stop=(k == K_BLOCKS - 1),
                 )
 
-        pooled = held.tile([P, M_BLOCKS, V], F32, name="pooled")
         for a in range(M_BLOCKS):
             z = held.tile([P, N], F32, name=f"z{a}")
             nc.scalar.activation(z[:], bank_tiles[a][:], tanh, bias=bias[:, a : a + 1])
+            pooled = held.tile([P, V], F32, name=f"pooled{a}")
             nc.vector.tensor_reduce(
-                pooled[:, a, :],
+                pooled[:],
                 z[:].rearrange("p (v t) -> p v t", t=D),
                 axis=mybir.AxisListType.X,
                 op=mybir.AluOpType.add,
             )
-
-        nc.vector.tensor_scalar_mul(pooled[:], pooled[:], 1.0 / D)
-        nc.sync.dma_start(out.rearrange("(a p) v -> p a v", p=P), pooled[:])
+            nc.vector.tensor_scalar_mul(pooled[:], pooled[:], 1.0 / D)
+            nc.sync.dma_start(out[a * P : (a + 1) * P, :], pooled[:])

@@ -56,12 +56,13 @@ def tile_gather_matmul_kernel(tc, table, w, b, offs, out):
         for a in range(M_BLOCKS):
             z = held.tile([P, N], F32, name=f"z{a}")
             nc.scalar.activation(z[:], bank_tiles[a][:], tanh, bias=bias[:, a : a + 1])
-            pooled = held.tile([P, V], F32, name=f"pooled{a}")
+            sums = held.tile([P, V], F32, name=f"sums{a}")
             nc.vector.tensor_reduce(
-                pooled[:],
+                sums[:],
                 z[:].rearrange("p (v t) -> p v t", t=D),
                 axis=mybir.AxisListType.X,
                 op=mybir.AluOpType.add,
             )
-            nc.vector.tensor_scalar_mul(pooled[:], pooled[:], 1.0 / D)
+            pooled = held.tile([P, V], F32, name=f"pooled{a}")
+            nc.scalar.mul(pooled[:], sums[:], 1.0 / D)
             nc.sync.dma_start(out[a * P : (a + 1) * P, :], pooled[:])

@@ -27,13 +27,12 @@ def tile_gather_matmul_kernel(tc, table, w, b, offs, out):
         offsets = held.tile([P, N // 16], U16, name="offsets")
         nc.sync.dma_start(offsets[:], offs)
 
-        bias = held.tile([P, M_BLOCKS], F32, name="bias")
-        with nc.allow_non_contiguous_dma(reason="one float32 to a partition for each block of b"):
-            nc.scalar.dma_start(bias[:], b.rearrange("(a p) o -> p (a o)", p=P))
-
         table_blocks = [held.tile([P, S], BF16, name=f"table{k}") for k in range(K_BLOCKS)]
         weight_blocks = [held.tile([P, M], BF16, name=f"weights{k}") for k in range(K_BLOCKS)]
         nc.scalar.dma_start(weight_blocks[0][:], w[0:P, :])
+        bias = held.tile([P, M_BLOCKS], F32, name="bias")
+        with nc.allow_non_contiguous_dma(reason="one float32 to a partition for each block of b"):
+            nc.scalar.dma_start(bias[:], b.rearrange("(a p) o -> p (a o)", p=P))
         nc.sync.dma_start(table_blocks[0][:], table[0:P, :])
         nc.sync.dma_start(weight_blocks[1][:], w[P : 2 * P, :])
         nc.sync.dma_start(table_blocks[1][:], table[P : 2 * P, :])

@@ -31,8 +31,7 @@ def tile_gather_matmul_kernel(tc, table, w, b, offs, out):
         weight_blocks = [held.tile([P, M], BF16, name=f"weights{k}") for k in range(K_BLOCKS)]
         nc.scalar.dma_start(weight_blocks[0][:], w[0:P, :])
         bias = held.tile([P, M_BLOCKS], F32, name="bias")
-        with nc.allow_non_contiguous_dma(reason="one float32 to a partition for each block of b"):
-            nc.scalar.dma_start(bias[:], b.rearrange("(a p) o -> p (a o)", p=P))
+        nc.scalar.dma_start(bias[:], b.rearrange("(p a) o -> p (a o)", a=M_BLOCKS))
         nc.sync.dma_start(table_blocks[0][:], table[0:P, :])
         nc.sync.dma_start(weight_blocks[1][:], w[P : 2 * P, :])
         nc.sync.dma_start(table_blocks[1][:], table[P : 2 * P, :])
@@ -46,22 +45,22 @@ def tile_gather_matmul_kernel(tc, table, w, b, offs, out):
             for a in range(M_BLOCKS):
                 nc.tensor.matmul(
                     bank_tiles[a][:],
-                    weight_blocks[k][:, a * P : (a + 1) * P],
+                    weight_blocks[k][:, a::M_BLOCKS],
                     table_blocks[k][:].indirect(offsets[:]),
                     start=(k == 0),
                     stop=(k == K_BLOCKS - 1),
                 )
 
+        sums = held.tile([P, M_BLOCKS * V], F32, name="sums")
         for a in range(M_BLOCKS):
             z = held.tile([P, N], F32, name=f"z{a}")
             nc.scalar.activation(z[:], bank_tiles[a][:], tanh, bias=bias[:, a : a + 1])
-            sums = held.tile([P, V], F32, name=f"sums{a}")
             nc.vector.tensor_reduce(
-                sums[:],
+                sums[:, a * V : (a + 1) * V],
                 z[:].rearrange("p (v t) -> p v t", t=D),
                 axis=mybir.AxisListType.X,
                 op=mybir.AluOpType.add,
             )
-            pooled = held.tile([P, V], F32, name=f"pooled{a}")
-            nc.scalar.mul(pooled[:], sums[:], 1.0 / D)
-            nc.sync.dma_start(out[a * P : (a + 1) * P, :], pooled[:])
+        pooled = held.tile([P, M_BLOCKS * V], F32, name="pooled")
+        nc.scalar.mul(pooled[:], sums[:], 1.0 / D)
+        nc.sync.dma_start(out.rearrange("(p a) v -> p (a v)", a=M_BLOCKS), pooled[:])

@@ -51,16 +51,17 @@ def tile_gather_matmul_kernel(tc, table, w, b, offs, out):
                     stop=(k == K_BLOCKS - 1),
                 )
 
-        sums = held.tile([P, M_BLOCKS * V], F32, name="sums")
+        out_rows = out.rearrange("(p a) v -> p a v", a=M_BLOCKS)
         for a in range(M_BLOCKS):
             z = held.tile([P, N], F32, name=f"z{a}")
             nc.scalar.activation(z[:], bank_tiles[a][:], tanh, bias=bias[:, a : a + 1])
+            sums = held.tile([P, V], F32, name=f"sums{a}")
             nc.vector.tensor_reduce(
-                sums[:, a * V : (a + 1) * V],
+                sums[:],
                 z[:].rearrange("p (v t) -> p v t", t=D),
                 axis=mybir.AxisListType.X,
                 op=mybir.AluOpType.add,
             )
-        pooled = held.tile([P, M_BLOCKS * V], F32, name="pooled")
-        nc.scalar.mul(pooled[:], sums[:], 1.0 / D)
-        nc.sync.dma_start(out.rearrange("(p a) v -> p (a v)", a=M_BLOCKS), pooled[:])
+            pooled = held.tile([P, V], F32, name=f"pooled{a}")
+            nc.scalar.mul(pooled[:], sums[:], 1.0 / D)
+            nc.sync.dma_start(out_rows[:, a, :], pooled[:])

@@ -13,6 +13,7 @@ D = 8
 V = N // D
 K_BLOCKS = K // P
 M_BLOCKS = M // P
+RUNS = 2
 
 FLOPS = 2 * K * M * N
 
@@ -54,14 +55,16 @@ def tile_gather_matmul_kernel(tc, table, w, b, offs, out):
         out_rows = out.rearrange("(p a) v -> p a v", a=M_BLOCKS)
         for a in range(M_BLOCKS):
             z = held.tile([P, N], F32, name=f"z{a}")
-            nc.scalar.activation(z[:], bank_tiles[a][:], tanh, bias=bias[:, a : a + 1])
             sums = held.tile([P, V], F32, name=f"sums{a}")
-            nc.vector.tensor_reduce(
-                sums[:],
-                z[:].rearrange("p (v t) -> p v t", t=D),
-                axis=mybir.AxisListType.X,
-                op=mybir.AluOpType.add,
-            )
+            for r in range(RUNS):
+                columns = slice(r * N // RUNS, (r + 1) * N // RUNS)
+                nc.scalar.activation(z[:, columns], bank_tiles[a][:, columns], tanh, bias=bias[:, a : a + 1])
+                nc.vector.tensor_reduce(
+                    sums[:, r * V // RUNS : (r + 1) * V // RUNS],
+                    z[:, columns].rearrange("p (v t) -> p v t", t=D),
+                    axis=mybir.AxisListType.X,
+                    op=mybir.AluOpType.add,
+                )
             pooled = held.tile([P, V], F32, name=f"pooled{a}")
             nc.scalar.mul(pooled[:], sums[:], 1.0 / D)
             nc.sync.dma_start(out_rows[:, a, :], pooled[:])

import concourse.mybir as mybir

BF16 = mybir.dt.bfloat16
F32 = mybir.dt.float32
U16 = mybir.dt.uint16

P = 128
S = 1024
K = 256
M = 256
N = 192
D = 8
V = N // D
K_BLOCKS = K // P
M_BLOCKS = M // P
RUNS = 2

FLOPS = 2 * K * M * N


def tile_gather_matmul_kernel(tc, table, w, b, offs, out):
    nc = tc.nc
    tanh = mybir.ActivationFunctionType.Tanh
    with (
        tc.tile_pool(name="held", bufs=1) as held,
        tc.psum_pool(name="banks", bufs=1) as banks,
    ):
        offsets = held.tile([P, N // 16], U16, name="offsets")
        nc.sync.dma_start(offsets[:], offs)

        table_blocks = [held.tile([P, S], BF16, name=f"table{k}") for k in range(K_BLOCKS)]
        weight_blocks = [held.tile([P, M], BF16, name=f"weights{k}") for k in range(K_BLOCKS)]
        nc.scalar.dma_start(weight_blocks[0][:], w[0:P, :])
        bias = held.tile([P, M_BLOCKS], F32, name="bias")
        nc.scalar.dma_start(bias[:], b.rearrange("(p a) o -> p (a o)", a=M_BLOCKS))
        nc.sync.dma_start(table_blocks[0][:], table[0:P, :])
        nc.sync.dma_start(weight_blocks[1][:], w[P : 2 * P, :])
        nc.sync.dma_start(table_blocks[1][:], table[P : 2 * P, :])

        scratch = held.tile([P, 1], F32, name="scratch")
        nc.vector.memset(scratch[:], 0.0)
        nc.scalar.activation(scratch[:], scratch[:], tanh)

        bank_tiles = [banks.tile([P, N], F32, name=f"bank{a}") for a in range(M_BLOCKS)]
        for k in range(K_BLOCKS):
            for a in range(M_BLOCKS):
                nc.tensor.matmul(
                    bank_tiles[a][:],
                    weight_blocks[k][:, a::M_BLOCKS],
                    table_blocks[k][:].indirect(offsets[:]),
                    start=(k == 0),
                    stop=(k == K_BLOCKS - 1),
                )

        out_rows = out.rearrange("(p a) v -> p a v", a=M_BLOCKS)
        for a in range(M_BLOCKS):
            z = held.tile([P, N], F32, name=f"z{a}")
            sums = held.tile([P, V], F32, name=f"sums{a}")
            for r in range(RUNS):
                columns = slice(r * N // RUNS, (r + 1) * N // RUNS)
                nc.scalar.activation(z[:, columns], bank_tiles[a][:, columns], tanh, bias=bias[:, a : a + 1])
                nc.vector.tensor_reduce(
                    sums[:, r * V // RUNS : (r + 1) * V // RUNS],
                    z[:, columns].rearrange("p (v t) -> p v t", t=D),
                    axis=mybir.AxisListType.X,
                    op=mybir.AluOpType.add,
                )
            pooled = held.tile([P, V], F32, name=f"pooled{a}")
            nc.scalar.mul(pooled[:], sums[:], 1.0 / D)
            nc.sync.dma_start(out_rows[:, a, :], pooled[:])
